import numpy as np
import ml_dtypes


def mxq(x, axis, fmt="e4m3"):
    dtype, down = {"e4m3": (ml_dtypes.float8_e4m3fn, 7), "e5m2": (ml_dtypes.float8_e5m2, 14)}[fmt]
    v = np.moveaxis(np.asarray(x, np.float32).astype(ml_dtypes.bfloat16).astype(np.float64), axis, -1)
    blocks = v.reshape(v.shape[:-1] + (-1, 32))
    amax = np.abs(blocks).max(-1, keepdims=True)
    byte = np.maximum(np.where(amax > 0, np.frexp(amax)[1] - 1 + 127, 0) - down, 1)
    scale = np.exp2(byte - 127.0)
    codes = (blocks / scale).astype(np.float32).astype(dtype).astype(np.float64)
    return np.moveaxis((codes * scale).reshape(v.shape), -1, axis)


WIDE = False


def mx_kscale(k):
    if not WIDE:
        return np.ones(k)
    levels = np.array([10, -10, 5, -5, 0])
    if k % 512:
        return np.exp2(np.random.permutation(np.resize(levels, k // 32))).repeat(32)
    a = np.empty((k // 512, 16))
    for p in range(k // 512):
        a[p, :8] = np.random.permutation(np.resize(levels, 8))
        for g in range(8):
            far = levels[np.abs(levels - a[p, g]) >= 10]
            a[p, g + 8] = far[np.random.randint(len(far))]
    return np.exp2(a.ravel()).repeat(32)


def f64(x):
    return np.asarray(x).astype(np.float64)


def striped(idx):
    return np.tile(idx.reshape(-1, 16).T, (8, 1)).astype(np.uint16)


def unstriped(offs):
    return offs[:16].T.reshape(-1).astype(np.int64)


def gelu(v):
    return 0.5 * v * (1.0 + np.tanh(np.sqrt(2.0 / np.pi) * (v + 0.044715 * v**3)))


K, T, E, C, H, N = 512, 2048, 8, 256, 1024, 128


def by_expert(wq, xq):
    return np.concatenate([wq[e].T @ xq[:, e * C:(e + 1) * C] for e in range(E)], axis=1)


def setup_inputs():
    n = np.random.standard_normal
    s = mx_kscale(K)[:, None]
    u = mx_kscale(H)
    return {
        "xT": (n((K, T)) * s).astype(np.float32),
        "w1": (n((E, K, H)) / np.sqrt(K) / s[None] * u[None, None, :]).astype(np.float32),
        "w2": (n((E, H, N)) / np.sqrt(H) / u[None, :, None]).astype(np.float32),
        "gate": np.tile(np.random.uniform(0.2, 1.0, E * C), (N, 1)).astype(np.float32),
        "offs": striped(np.random.permutation(T)[:E * C]),
    }


def reference(xT, w1, w2, gate, offs):
    idx = unstriped(offs)
    xq = mxq(f64(xT)[:, idx], 0, "e4m3")
    h = gelu(by_expert(mxq(f64(w1), 1, "e4m3"), xq))
    y = by_expert(mxq(f64(w2), 1, "e4m3"), mxq(h, 0, "e4m3"))
    out = np.zeros((N, T))
    out[:, idx] = f64(gate) * y
    return out

@@ -1,0 +1,235 @@
+from contextlib import ExitStack
+
+import concourse.mybir as mybir
+
+K, T, E, C, H, N = 512, 2048, 8, 256, 1024, 128
+P = 128
+PACK = 4
+G = H // 512
+MT = 128
+FLOPS = 2 * E * C * (K * H + H * N)
+
+F32 = mybir.dt.float32
+BF16 = mybir.dt.bfloat16
+U32 = mybir.dt.uint32
+U16 = mybir.dt.uint16
+U8 = mybir.dt.uint8
+FP8X4 = mybir.dt.float8_e4m3fn_x4
+ACT = mybir.ActivationFunctionType
+MULT = mybir.AluOpType.mult
+ADD = mybir.AluOpType.add
+
+X_CHUNK = 512
+X_VECTOR = 352
+W1_VECTOR = 60
+
+
+def tile_routed_moe_kernel(tc, xT, w1, w2, gate, offs, out):
+    nc = tc.nc
+    with ExitStack() as ctx:
+        keep = ctx.enter_context(tc.tile_pool(name="keep", bufs=1))
+        xraw_pool = ctx.enter_context(tc.tile_pool(name="xraw", bufs=T // X_CHUNK))
+        w1raw_pool = ctx.enter_context(tc.tile_pool(name="w1raw", bufs=4))
+        w2raw_pool = ctx.enter_context(tc.tile_pool(name="w2raw", bufs=3))
+        stage = ctx.enter_context(tc.tile_pool(name="stage", bufs=3))
+        xstage = ctx.enter_context(tc.tile_pool(name="xstage", bufs=2))
+        spool = ctx.enter_context(tc.tile_pool(name="slots", bufs=2))
+        hpool = ctx.enter_context(tc.tile_pool(name="hid", bufs=3))
+        psum_h = ctx.enter_context(tc.psum_pool(name="psum_h", bufs=6))
+        psum_y = ctx.enter_context(tc.psum_pool(name="psum_y", bufs=2))
+
+        offsets = keep.tile([P, E * C // 16], U16, name="offsets")
+        x_codes = keep.tile([P, T], U32, name="x_codes", align_bytes=64)
+        x_scales = keep.tile([P, T], U8, name="x_scales", align_bytes=64)
+        gates = keep.tile([P, E * C], F32, name="gates")
+        result = keep.tile([P, T], F32, name="result")
+        warm = keep.tile([P, 1], F32, name="warm")
+
+        nc.vector.memset(warm[:], 0.0)
+        nc.scalar.activation(warm[:], warm[:], ACT.Gelu_apprx_tanh)
+
+        def gpsimd_copy(dst, src):
+            nc.gpsimd.tensor_scalar(dst, src, 1.0, 0.0, MULT, ADD)
+
+        engines = {"V": nc.vector.tensor_copy, "S": nc.scalar.copy, "G": gpsimd_copy}
+
+        x_rows = xT.rearrange("(p t) n -> p t n", t=PACK)
+        x_raw = {}
+        w1_raw = {}
+        w2_raw = {}
+
+        def load_x(a):
+            raw = xraw_pool.tile([P, PACK, X_CHUNK], F32, name="x_raw")
+            nc.sync.dma_start(raw[:], x_rows[:, :, a * X_CHUNK : (a + 1) * X_CHUNK])
+            x_raw[a] = raw
+
+        def load_w1(e, pieces=1):
+            raw = w1raw_pool.tile([P, PACK, H], F32, name="w1_raw")
+            rows = w1[e].rearrange("(p j) c -> p j c", j=PACK)
+            width = H // pieces
+            for i in range(pieces):
+                nc.sync.dma_start(raw[:, :, i * width : (i + 1) * width], rows[:, :, i * width : (i + 1) * width])
+            w1_raw[e] = raw
+
+        def load_w2(e):
+            raw = w2raw_pool.tile([P, G, PACK, N], F32, name="w2_raw")
+            nc.sync.dma_start(raw[:], w2[e].rearrange("(g p j) n -> p g j n", g=G, j=PACK))
+            w2_raw[e] = raw
+
+        def load_gate(a, b):
+            nc.sync.dma_start(gates[:, a * C : b * C], gate[:, a * C : b * C])
+
+        def tokens(a, split):
+            raw = x_raw[a]
+            grouped = xstage.tile([P, X_CHUNK, PACK], BF16, name="x_grouped", align_bytes=64)
+            for eng, lo, hi in split:
+                engines[eng](
+                    grouped[:, lo:hi, :].rearrange("p (c i) t -> p c t i", i=4),
+                    raw[:, :, lo:hi].rearrange("p t (c i) -> p c t i", i=4),
+                )
+            nc.vector.quantize_mx(
+                out=x_codes[:, a * X_CHUNK : (a + 1) * X_CHUNK].bitcast(FP8X4),
+                scales=x_scales[:, a * X_CHUNK : (a + 1) * X_CHUNK],
+                in_=grouped[:].rearrange("p n t -> p (n t)"),
+            )
+
+        w1_codes = {}
+        w2_codes = {}
+
+        def quantise_w1(e, copies, quants=1):
+            raw = w1_raw[e][:].rearrange("p j (g m t) -> p g m j t", g=G, t=PACK)
+            codes = stage.tile([P, H], U32, name="w1_codes", align_bytes=64)
+            scales = stage.tile([P, H], U8, name="w1_scales", align_bytes=64)
+            grouped = stage.tile([P, G, PACK, MT, PACK], BF16, name="w1_grouped", align_bytes=64)
+            dst = grouped[:].rearrange("p g t m j -> p g m j t")
+            for eng, g0, g1, m0, m1 in copies:
+                if g1 - g0 == 1:
+                    engines[eng](dst[:, g0, m0:m1], raw[:, g0, m0:m1])
+                else:
+                    engines[eng](dst[:, g0:g1, m0:m1], raw[:, g0:g1, m0:m1])
+            flat = grouped[:].rearrange("p g t m j -> p (g t m j)")
+            width = H // quants
+            for i in range(quants):
+                nc.vector.quantize_mx(
+                    out=codes[:, i * width : (i + 1) * width].bitcast(FP8X4),
+                    scales=scales[:, i * width : (i + 1) * width],
+                    in_=flat[:, i * width * PACK : (i + 1) * width * PACK],
+                )
+            w1_codes[e] = (codes, scales)
+
+        def quantise_w2(e, eng):
+            grouped = stage.tile([P, G, N, PACK], BF16, name="w2_grouped", align_bytes=64)
+            codes = stage.tile([P, G * N], U32, name="w2_codes", align_bytes=64)
+            scales = stage.tile([P, G * N], U8, name="w2_scales", align_bytes=64)
+            engines[eng](
+                grouped[:].rearrange("p g (c i) j -> p g c j i", i=4),
+                w2_raw[e][:].rearrange("p g j (c i) -> p g c j i", i=4),
+            )
+            nc.vector.quantize_mx(
+                out=codes[:].bitcast(FP8X4),
+                scales=scales[:],
+                in_=grouped[:].rearrange("p g n j -> p (g n j)"),
+            )
+            w2_codes[e] = (codes, scales)
+
+        slots_of = {}
+
+        def gather(e):
+            lst = offsets[:, e * C // 16 : (e + 1) * C // 16]
+            slot_codes = spool.tile([P, C], U32, name="slot_codes", align_bytes=64)
+            slot_scales = spool.tile([P, C], U8, name="slot_scales", align_bytes=64)
+            nc.vector.tensor_copy(slot_codes[:], x_codes[:].indirect(lst))
+            nc.vector.tensor_copy(slot_scales[:], x_scales[:].indirect(lst))
+            slots_of[e] = (slot_codes, slot_scales)
+
+        hidden_of = {}
+        h_codes = {}
+
+        def layer1(e):
+            codes, scales = w1_codes[e]
+            slot_codes, slot_scales = slots_of[e]
+            hidden = hpool.tile([P, G, C, PACK], BF16, name="hidden", align_bytes=64)
+            for g in range(G):
+                for s in range(C // MT):
+                    slots = slice(s * MT, (s + 1) * MT)
+                    acc = psum_h.tile([P, PACK, MT], F32, name="acc_h")
+                    for t in range(PACK):
+                        chans = slice(g * 512 + t * MT, g * 512 + (t + 1) * MT)
+                        nc.tensor.matmul_mx(
+                            out=acc[:, t, :],
+                            lhsT=codes[:, chans].bitcast(FP8X4),
+                            lhsT_scale=scales[:, chans],
+                            rhs=slot_codes[:, slots].bitcast(FP8X4),
+                            rhs_scale=slot_scales[:, slots],
+                            start=True,
+                            stop=True,
+                        )
+                    nc.scalar.activation(
+                        hidden[:, g, s * MT : (s + 1) * MT, :],
+                        acc[:].rearrange("p t n -> p n t"),
+                        ACT.Gelu_apprx_tanh,
+                    )
+            hidden_of[e] = hidden
+
+        def quantise_h(e, quants=1):
+            flat = hidden_of[e][:].rearrange("p g n t -> p (g n t)")
+            hc = hpool.tile([P, G * C], U32, name="h_codes", align_bytes=64)
+            hs = hpool.tile([P, G * C], U8, name="h_scales", align_bytes=64)
+            width = G * C // quants
+            for i in range(quants):
+                nc.vector.quantize_mx(
+                    out=hc[:, i * width : (i + 1) * width].bitcast(FP8X4),
+                    scales=hs[:, i * width : (i + 1) * width],
+                    in_=flat[:, i * width * PACK : (i + 1) * width * PACK],
+                )
+            h_codes[e] = (hc, hs)
+
+        def layer2(e):
+            codes, scales = w2_codes[e]
+            hc, hs = h_codes[e]
+            acc = psum_y.tile([P, C], F32, name="acc_y")
+            for g in range(G):
+                nc.tensor.matmul_mx(
+                    out=acc[:],
+                    lhsT=codes[:, g * N : (g + 1) * N].bitcast(FP8X4),
+                    lhsT_scale=scales[:, g * N : (g + 1) * N],
+                    rhs=hc[:, g * C : (g + 1) * C].bitcast(FP8X4),
+                    rhs_scale=hs[:, g * C : (g + 1) * C],
+                    start=(g == 0),
+                    stop=(g == G - 1),
+                )
+            y = hpool.tile([P, C], F32, name="y")
+            lst = offsets[:, e * C // 16 : (e + 1) * C // 16]
+            nc.scalar.copy(y[:], acc[:])
+            nc.vector.tensor_tensor(result[:].indirect(lst), y[:], gates[:, e * C : (e + 1) * C], MULT)
+
+        nc.sync.dma_start(offsets[:], offs)
+        for a in range(T // X_CHUNK):
+            load_x(a)
+        load_w1(0, 2)
+        load_w2(0)
+        load_w1(1)
+        load_gate(0, 4)
+        load_w2(1)
+        load_w1(2)
+        load_w2(2)
+        load_w1(3)
+        for a in range(T // X_CHUNK):
+            tokens(a, (("V", 0, X_VECTOR), ("S", X_VECTOR, X_CHUNK)))
+        for e in range(E):
+            gather(e)
+            if e == 0:
+                quantise_w1(e, (("S", 0, 1, W1_VECTOR, MT), ("V", 0, 1, 0, W1_VECTOR), ("S", 1, 2, W1_VECTOR, MT), ("V", 1, 2, 0, W1_VECTOR)), 2)
+            else:
+                quantise_w1(e, (("S", 0, 2, W1_VECTOR, MT), ("V", 0, 2, 0, W1_VECTOR)))
+            quantise_w2(e, "S")
+            if e + 3 < E:
+                load_w2(e + 3)
+            if e + 4 < E:
+                load_w1(e + 4)
+            if e == 1:
+                load_gate(4, 8)
+            layer1(e)
+            quantise_h(e)
+            layer2(e)
+        nc.sync.dma_start(out, result[:])

@@ -20,8 +20,7 @@ MULT = mybir.AluOpType.mult
 ADD = mybir.AluOpType.add
 
 X_CHUNK = 512
-X_VECTOR = 352
-W1_VECTOR = 60
+X_VECTOR = 288
 
 
 def tile_routed_moe_kernel(tc, xT, w1, w2, gate, offs, out):
@@ -30,7 +29,7 @@ def tile_routed_moe_kernel(tc, xT, w1, w2, gate, offs, out):
         keep = ctx.enter_context(tc.tile_pool(name="keep", bufs=1))
         xraw_pool = ctx.enter_context(tc.tile_pool(name="xraw", bufs=T // X_CHUNK))
         w1raw_pool = ctx.enter_context(tc.tile_pool(name="w1raw", bufs=4))
-        w2raw_pool = ctx.enter_context(tc.tile_pool(name="w2raw", bufs=3))
+        w2raw_pool = ctx.enter_context(tc.tile_pool(name="w2raw", bufs=4))
         stage = ctx.enter_context(tc.tile_pool(name="stage", bufs=3))
         xstage = ctx.enter_context(tc.tile_pool(name="xstage", bufs=2))
         spool = ctx.enter_context(tc.tile_pool(name="slots", bufs=2))
@@ -134,24 +133,26 @@ def tile_routed_moe_kernel(tc, xT, w1, w2, gate, offs, out):
 
         slots_of = {}
 
-        def gather(e):
-            lst = offsets[:, e * C // 16 : (e + 1) * C // 16]
-            slot_codes = spool.tile([P, C], U32, name="slot_codes", align_bytes=64)
-            slot_scales = spool.tile([P, C], U8, name="slot_scales", align_bytes=64)
-            nc.vector.tensor_copy(slot_codes[:], x_codes[:].indirect(lst))
-            nc.vector.tensor_copy(slot_scales[:], x_scales[:].indirect(lst))
-            slots_of[e] = (slot_codes, slot_scales)
+        def gather(first, count):
+            n = count * C
+            lst = offsets[:, first * C // 16 : (first * C + n) // 16]
+            slot_codes = spool.tile([P, 2 * C], U32, name="slot_codes", align_bytes=64)
+            slot_scales = spool.tile([P, 2 * C], U8, name="slot_scales", align_bytes=64)
+            nc.vector.tensor_copy(slot_codes[:, 0:n], x_codes[:].indirect(lst))
+            nc.vector.tensor_copy(slot_scales[:, 0:n], x_scales[:].indirect(lst))
+            for i in range(count):
+                slots_of[first + i] = (slot_codes, slot_scales, i * C)
 
         hidden_of = {}
         h_codes = {}
 
         def layer1(e):
             codes, scales = w1_codes[e]
-            slot_codes, slot_scales = slots_of[e]
+            slot_codes, slot_scales, base = slots_of[e]
             hidden = hpool.tile([P, G, C, PACK], BF16, name="hidden", align_bytes=64)
             for g in range(G):
                 for s in range(C // MT):
-                    slots = slice(s * MT, (s + 1) * MT)
+                    slots = slice(base + s * MT, base + (s + 1) * MT)
                     acc = psum_h.tile([P, PACK, MT], F32, name="acc_h")
                     for t in range(PACK):
                         chans = slice(g * 512 + t * MT, g * 512 + (t + 1) * MT)
@@ -184,13 +185,18 @@ def tile_routed_moe_kernel(tc, xT, w1, w2, gate, offs, out):
                 )
             h_codes[e] = (hc, hs)
 
-        def layer2(e):
+        group = {}
+
+        def layer2(e, first, count):
             codes, scales = w2_codes[e]
             hc, hs = h_codes[e]
-            acc = psum_y.tile([P, C], F32, name="acc_y")
+            if e == first:
+                group["acc"] = psum_y.tile([P, 2 * C], F32, name="acc_y")
+            acc = group["acc"]
+            cols = slice((e - first) * C, (e - first + 1) * C)
             for g in range(G):
                 nc.tensor.matmul_mx(
-                    out=acc[:],
+                    out=acc[:, cols],
                     lhsT=codes[:, g * N : (g + 1) * N].bitcast(FP8X4),
                     lhsT_scale=scales[:, g * N : (g + 1) * N],
                     rhs=hc[:, g * C : (g + 1) * C].bitcast(FP8X4),
@@ -198,38 +204,67 @@ def tile_routed_moe_kernel(tc, xT, w1, w2, gate, offs, out):
                     start=(g == 0),
                     stop=(g == G - 1),
                 )
-            y = hpool.tile([P, C], F32, name="y")
-            lst = offsets[:, e * C // 16 : (e + 1) * C // 16]
-            nc.scalar.copy(y[:], acc[:])
-            nc.vector.tensor_tensor(result[:].indirect(lst), y[:], gates[:, e * C : (e + 1) * C], MULT)
+            if e == first + count - 1:
+                n = count * C
+                y = hpool.tile([P, 2 * C], F32, name="y")
+                lst = offsets[:, first * C // 16 : (first * C + n) // 16]
+                slots = slice(first * C, first * C + n)
+                nc.scalar.copy(y[:, 0:n], acc[:, 0:n])
+                nc.vector.tensor_tensor(result[:].indirect(lst), y[:, 0:n], gates[:, slots], MULT)
 
         nc.sync.dma_start(offsets[:], offs)
-        for a in range(T // X_CHUNK):
-            load_x(a)
-        load_w1(0, 2)
+        load_x(0)
+        load_x(1)
+        load_x(2)
+        load_x(3)
         load_w2(0)
-        load_w1(1)
-        load_gate(0, 4)
         load_w2(1)
-        load_w1(2)
         load_w2(2)
-        load_w1(3)
+        load_w2(3)
+        load_w1(0, 2)
+        load_w1(1, 2)
+        load_w1(2, 2)
+        load_gate(0, 4)
+        load_w1(3, 1)
+        load_w1(4, 1)
+        load_w1(5, 1)
+        load_w2(4)
+        load_w1(6, 2)
+        load_w1(7, 2)
+        load_w2(5)
+        load_w2(6)
+        load_w2(7)
+        load_gate(4, 8)
         for a in range(T // X_CHUNK):
             tokens(a, (("V", 0, X_VECTOR), ("S", X_VECTOR, X_CHUNK)))
-        for e in range(E):
-            gather(e)
-            if e == 0:
-                quantise_w1(e, (("S", 0, 1, W1_VECTOR, MT), ("V", 0, 1, 0, W1_VECTOR), ("S", 1, 2, W1_VECTOR, MT), ("V", 1, 2, 0, W1_VECTOR)), 2)
-            else:
-                quantise_w1(e, (("S", 0, 2, W1_VECTOR, MT), ("V", 0, 2, 0, W1_VECTOR)))
-            quantise_w2(e, "S")
-            if e + 3 < E:
-                load_w2(e + 3)
-            if e + 4 < E:
-                load_w1(e + 4)
-            if e == 1:
-                load_gate(4, 8)
-            layer1(e)
-            quantise_h(e)
-            layer2(e)
+        vector_share = (32, 88, 32, 32, 16, 104, 40, 128)
+        fine = (1, 1, 1, 0, 0, 0, 1, 1)
+        fine_h = (1, 0, 1, 0, 0, 1, 0, 1)
+        gathers = {0: 2, 2: 2, 4: 2, 6: 2}
+        scatters = ((0, 2), (0, 2), (2, 1), (3, 1), (4, 1), (5, 1), (6, 1), (7, 1))
+
+        def stage_gather(e):
+            if e in gathers:
+                gather(e, gathers[e])
+
+        def stage_w1(e):
+            v = vector_share[e]
+            groups = [(0, 1), (1, 2)] if fine[e] else [(0, 2)]
+            cuts = [("S", v, MT), ("V", 0, v)]
+            quantise_w1(e, [(eng, lo, hi, m0, m1) for lo, hi in groups for eng, m0, m1 in cuts if m0 < m1], len(groups))
+
+        steps = {
+            "g": stage_gather,
+            "1": stage_w1,
+            "2": lambda e: quantise_w2(e, "SSSSSSSS"[e]),
+            "L": layer1,
+            "h": lambda e: quantise_h(e, 2 if fine_h[e] else 1),
+            "y": lambda e: layer2(e, *scatters[e]),
+        }
+        lags = {"1": 0, "2": 0, "g": 0, "L": 1, "h": 1, "y": 2}
+        for i in range(E + 3):
+            for step in "gL1yh2":
+                e = i - lags[step]
+                if 0 <= e < E:
+                    steps[step](e)
         nc.sync.dma_start(out, result[:])

@@ -20,7 +20,6 @@ MULT = mybir.AluOpType.mult
 ADD = mybir.AluOpType.add
 
 X_CHUNK = 512
-X_VECTOR = 288
 
 
 def tile_routed_moe_kernel(tc, xT, w1, w2, gate, offs, out):
@@ -32,7 +31,7 @@ def tile_routed_moe_kernel(tc, xT, w1, w2, gate, offs, out):
         w2raw_pool = ctx.enter_context(tc.tile_pool(name="w2raw", bufs=4))
         stage = ctx.enter_context(tc.tile_pool(name="stage", bufs=3))
         xstage = ctx.enter_context(tc.tile_pool(name="xstage", bufs=2))
-        spool = ctx.enter_context(tc.tile_pool(name="slots", bufs=2))
+        spool = ctx.enter_context(tc.tile_pool(name="slots", bufs=3))
         hpool = ctx.enter_context(tc.tile_pool(name="hid", bufs=3))
         psum_h = ctx.enter_context(tc.psum_pool(name="psum_h", bufs=6))
         psum_y = ctx.enter_context(tc.psum_pool(name="psum_y", bufs=2))
@@ -214,34 +213,35 @@ def tile_routed_moe_kernel(tc, xT, w1, w2, gate, offs, out):
 
         nc.sync.dma_start(offsets[:], offs)
         load_x(0)
+        load_w2(0)
         load_x(1)
         load_x(2)
         load_x(3)
-        load_w2(0)
         load_w2(1)
-        load_w2(2)
-        load_w2(3)
         load_w1(0, 2)
+        load_w2(2)
         load_w1(1, 2)
-        load_w1(2, 2)
         load_gate(0, 4)
-        load_w1(3, 1)
+        load_w2(3)
+        load_w1(2, 1)
+        load_w1(3, 2)
         load_w1(4, 1)
-        load_w1(5, 1)
+        load_w1(5, 2)
         load_w2(4)
         load_w1(6, 2)
-        load_w1(7, 2)
+        load_w1(7, 1)
+        load_gate(4, 8)
         load_w2(5)
         load_w2(6)
         load_w2(7)
-        load_gate(4, 8)
+        x_vector = (128, 192, 192, 192)
         for a in range(T // X_CHUNK):
-            tokens(a, (("V", 0, X_VECTOR), ("S", X_VECTOR, X_CHUNK)))
-        vector_share = (32, 88, 32, 32, 16, 104, 40, 128)
-        fine = (1, 1, 1, 0, 0, 0, 1, 1)
-        fine_h = (1, 0, 1, 0, 0, 1, 0, 1)
-        gathers = {0: 2, 2: 2, 4: 2, 6: 2}
-        scatters = ((0, 2), (0, 2), (2, 1), (3, 1), (4, 1), (5, 1), (6, 1), (7, 1))
+            tokens(a, (("V", 0, x_vector[a]), ("S", x_vector[a], X_CHUNK)))
+        vector_share = (16, 64, 32, 88, 48, 80, 88, 64)
+        fine = (1, 1, 0, 1, 0, 1, 1, 0)
+        fine_h = (1, 1, 0, 1, 1, 0, 1, 0)
+        gathers = {0: 1, 1: 2, 3: 1, 4: 1, 5: 2, 7: 1}
+        scatters = ((0, 1), (1, 2), (1, 2), (3, 1), (4, 1), (5, 1), (6, 1), (7, 1))
 
         def stage_gather(e):
             if e in gathers:
@@ -256,14 +256,14 @@ def tile_routed_moe_kernel(tc, xT, w1, w2, gate, offs, out):
         steps = {
             "g": stage_gather,
             "1": stage_w1,
-            "2": lambda e: quantise_w2(e, "SSSSSSSS"[e]),
+            "2": lambda e: quantise_w2(e, "VVVVSSVV"[e]),
             "L": layer1,
             "h": lambda e: quantise_h(e, 2 if fine_h[e] else 1),
             "y": lambda e: layer2(e, *scatters[e]),
         }
-        lags = {"1": 0, "2": 0, "g": 0, "L": 1, "h": 1, "y": 2}
+        lags = {"1": 0, "2": 0, "g": 0, "L": 1, "h": 2, "y": 2}
         for i in range(E + 3):
-            for step in "gL1yh2":
+            for step in "g21hLy":
                 e = i - lags[step]
                 if 0 <= e < E:
                     steps[step](e)

from contextlib import ExitStack

import concourse.mybir as mybir

K, T, E, C, H, N = 512, 2048, 8, 256, 1024, 128
P = 128
PACK = 4
G = H // 512
MT = 128
FLOPS = 2 * E * C * (K * H + H * N)

F32 = mybir.dt.float32
BF16 = mybir.dt.bfloat16
U32 = mybir.dt.uint32
U16 = mybir.dt.uint16
U8 = mybir.dt.uint8
FP8X4 = mybir.dt.float8_e4m3fn_x4
ACT = mybir.ActivationFunctionType
MULT = mybir.AluOpType.mult
ADD = mybir.AluOpType.add

X_CHUNK = 512


def tile_routed_moe_kernel(tc, xT, w1, w2, gate, offs, out):
    nc = tc.nc
    with ExitStack() as ctx:
        keep = ctx.enter_context(tc.tile_pool(name="keep", bufs=1))
        xraw_pool = ctx.enter_context(tc.tile_pool(name="xraw", bufs=T // X_CHUNK))
        w1raw_pool = ctx.enter_context(tc.tile_pool(name="w1raw", bufs=4))
        w2raw_pool = ctx.enter_context(tc.tile_pool(name="w2raw", bufs=4))
        stage = ctx.enter_context(tc.tile_pool(name="stage", bufs=3))
        xstage = ctx.enter_context(tc.tile_pool(name="xstage", bufs=2))
        spool = ctx.enter_context(tc.tile_pool(name="slots", bufs=3))
        hpool = ctx.enter_context(tc.tile_pool(name="hid", bufs=3))
        psum_h = ctx.enter_context(tc.psum_pool(name="psum_h", bufs=6))
        psum_y = ctx.enter_context(tc.psum_pool(name="psum_y", bufs=2))

        offsets = keep.tile([P, E * C // 16], U16, name="offsets")
        x_codes = keep.tile([P, T], U32, name="x_codes", align_bytes=64)
        x_scales = keep.tile([P, T], U8, name="x_scales", align_bytes=64)
        gates = keep.tile([P, E * C], F32, name="gates")
        result = keep.tile([P, T], F32, name="result")
        warm = keep.tile([P, 1], F32, name="warm")

        nc.vector.memset(warm[:], 0.0)
        nc.scalar.activation(warm[:], warm[:], ACT.Gelu_apprx_tanh)

        def gpsimd_copy(dst, src):
            nc.gpsimd.tensor_scalar(dst, src, 1.0, 0.0, MULT, ADD)

        engines = {"V": nc.vector.tensor_copy, "S": nc.scalar.copy, "G": gpsimd_copy}

        x_rows = xT.rearrange("(p t) n -> p t n", t=PACK)
        x_raw = {}
        w1_raw = {}
        w2_raw = {}

        def load_x(a):
            raw = xraw_pool.tile([P, PACK, X_CHUNK], F32, name="x_raw")
            nc.sync.dma_start(raw[:], x_rows[:, :, a * X_CHUNK : (a + 1) * X_CHUNK])
            x_raw[a] = raw

        def load_w1(e, pieces=1):
            raw = w1raw_pool.tile([P, PACK, H], F32, name="w1_raw")
            rows = w1[e].rearrange("(p j) c -> p j c", j=PACK)
            width = H // pieces
            for i in range(pieces):
                nc.sync.dma_start(raw[:, :, i * width : (i + 1) * width], rows[:, :, i * width : (i + 1) * width])
            w1_raw[e] = raw

        def load_w2(e):
            raw = w2raw_pool.tile([P, G, PACK, N], F32, name="w2_raw")
            nc.sync.dma_start(raw[:], w2[e].rearrange("(g p j) n -> p g j n", g=G, j=PACK))
            w2_raw[e] = raw

        def load_gate(a, b):
            nc.sync.dma_start(gates[:, a * C : b * C], gate[:, a * C : b * C])

        def tokens(a, split):
            raw = x_raw[a]
            grouped = xstage.tile([P, X_CHUNK, PACK], BF16, name="x_grouped", align_bytes=64)
            for eng, lo, hi in split:
                engines[eng](
                    grouped[:, lo:hi, :].rearrange("p (c i) t -> p c t i", i=4),
                    raw[:, :, lo:hi].rearrange("p t (c i) -> p c t i", i=4),
                )
            nc.vector.quantize_mx(
                out=x_codes[:, a * X_CHUNK : (a + 1) * X_CHUNK].bitcast(FP8X4),
                scales=x_scales[:, a * X_CHUNK : (a + 1) * X_CHUNK],
                in_=grouped[:].rearrange("p n t -> p (n t)"),
            )

        w1_codes = {}
        w2_codes = {}

        def quantise_w1(e, copies, quants=1):
            raw = w1_raw[e][:].rearrange("p j (g m t) -> p g m j t", g=G, t=PACK)
            codes = stage.tile([P, H], U32, name="w1_codes", align_bytes=64)
            scales = stage.tile([P, H], U8, name="w1_scales", align_bytes=64)
            grouped = stage.tile([P, G, PACK, MT, PACK], BF16, name="w1_grouped", align_bytes=64)
            dst = grouped[:].rearrange("p g t m j -> p g m j t")
            for eng, g0, g1, m0, m1 in copies:
                if g1 - g0 == 1:
                    engines[eng](dst[:, g0, m0:m1], raw[:, g0, m0:m1])
                else:
                    engines[eng](dst[:, g0:g1, m0:m1], raw[:, g0:g1, m0:m1])
            flat = grouped[:].rearrange("p g t m j -> p (g t m j)")
            width = H // quants
            for i in range(quants):
                nc.vector.quantize_mx(
                    out=codes[:, i * width : (i + 1) * width].bitcast(FP8X4),
                    scales=scales[:, i * width : (i + 1) * width],
                    in_=flat[:, i * width * PACK : (i + 1) * width * PACK],
                )
            w1_codes[e] = (codes, scales)

        def quantise_w2(e, eng):
            grouped = stage.tile([P, G, N, PACK], BF16, name="w2_grouped", align_bytes=64)
            codes = stage.tile([P, G * N], U32, name="w2_codes", align_bytes=64)
            scales = stage.tile([P, G * N], U8, name="w2_scales", align_bytes=64)
            engines[eng](
                grouped[:].rearrange("p g (c i) j -> p g c j i", i=4),
                w2_raw[e][:].rearrange("p g j (c i) -> p g c j i", i=4),
            )
            nc.vector.quantize_mx(
                out=codes[:].bitcast(FP8X4),
                scales=scales[:],
                in_=grouped[:].rearrange("p g n j -> p (g n j)"),
            )
            w2_codes[e] = (codes, scales)

        slots_of = {}

        def gather(first, count):
            n = count * C
            lst = offsets[:, first * C // 16 : (first * C + n) // 16]
            slot_codes = spool.tile([P, 2 * C], U32, name="slot_codes", align_bytes=64)
            slot_scales = spool.tile([P, 2 * C], U8, name="slot_scales", align_bytes=64)
            nc.vector.tensor_copy(slot_codes[:, 0:n], x_codes[:].indirect(lst))
            nc.vector.tensor_copy(slot_scales[:, 0:n], x_scales[:].indirect(lst))
            for i in range(count):
                slots_of[first + i] = (slot_codes, slot_scales, i * C)

        hidden_of = {}
        h_codes = {}

        def layer1(e):
            codes, scales = w1_codes[e]
            slot_codes, slot_scales, base = slots_of[e]
            hidden = hpool.tile([P, G, C, PACK], BF16, name="hidden", align_bytes=64)
            for g in range(G):
                for s in range(C // MT):
                    slots = slice(base + s * MT, base + (s + 1) * MT)
                    acc = psum_h.tile([P, PACK, MT], F32, name="acc_h")
                    for t in range(PACK):
                        chans = slice(g * 512 + t * MT, g * 512 + (t + 1) * MT)
                        nc.tensor.matmul_mx(
                            out=acc[:, t, :],
                            lhsT=codes[:, chans].bitcast(FP8X4),
                            lhsT_scale=scales[:, chans],
                            rhs=slot_codes[:, slots].bitcast(FP8X4),
                            rhs_scale=slot_scales[:, slots],
                            start=True,
                            stop=True,
                        )
                    nc.scalar.activation(
                        hidden[:, g, s * MT : (s + 1) * MT, :],
                        acc[:].rearrange("p t n -> p n t"),
                        ACT.Gelu_apprx_tanh,
                    )
            hidden_of[e] = hidden

        def quantise_h(e, quants=1):
            flat = hidden_of[e][:].rearrange("p g n t -> p (g n t)")
            hc = hpool.tile([P, G * C], U32, name="h_codes", align_bytes=64)
            hs = hpool.tile([P, G * C], U8, name="h_scales", align_bytes=64)
            width = G * C // quants
            for i in range(quants):
                nc.vector.quantize_mx(
                    out=hc[:, i * width : (i + 1) * width].bitcast(FP8X4),
                    scales=hs[:, i * width : (i + 1) * width],
                    in_=flat[:, i * width * PACK : (i + 1) * width * PACK],
                )
            h_codes[e] = (hc, hs)

        group = {}

        def layer2(e, first, count):
            codes, scales = w2_codes[e]
            hc, hs = h_codes[e]
            if e == first:
                group["acc"] = psum_y.tile([P, 2 * C], F32, name="acc_y")
            acc = group["acc"]
            cols = slice((e - first) * C, (e - first + 1) * C)
            for g in range(G):
                nc.tensor.matmul_mx(
                    out=acc[:, cols],
                    lhsT=codes[:, g * N : (g + 1) * N].bitcast(FP8X4),
                    lhsT_scale=scales[:, g * N : (g + 1) * N],
                    rhs=hc[:, g * C : (g + 1) * C].bitcast(FP8X4),
                    rhs_scale=hs[:, g * C : (g + 1) * C],
                    start=(g == 0),
                    stop=(g == G - 1),
                )
            if e == first + count - 1:
                n = count * C
                y = hpool.tile([P, 2 * C], F32, name="y")
                lst = offsets[:, first * C // 16 : (first * C + n) // 16]
                slots = slice(first * C, first * C + n)
                nc.scalar.copy(y[:, 0:n], acc[:, 0:n])
                nc.vector.tensor_tensor(result[:].indirect(lst), y[:, 0:n], gates[:, slots], MULT)

        nc.sync.dma_start(offsets[:], offs)
        load_x(0)
        load_w2(0)
        load_x(1)
        load_x(2)
        load_x(3)
        load_w2(1)
        load_w1(0, 2)
        load_w2(2)
        load_w1(1, 2)
        load_gate(0, 4)
        load_w2(3)
        load_w1(2, 1)
        load_w1(3, 2)
        load_w1(4, 1)
        load_w1(5, 2)
        load_w2(4)
        load_w1(6, 2)
        load_w1(7, 1)
        load_gate(4, 8)
        load_w2(5)
        load_w2(6)
        load_w2(7)
        x_vector = (128, 192, 192, 192)
        for a in range(T // X_CHUNK):
            tokens(a, (("V", 0, x_vector[a]), ("S", x_vector[a], X_CHUNK)))
        vector_share = (16, 64, 32, 88, 48, 80, 88, 64)
        fine = (1, 1, 0, 1, 0, 1, 1, 0)
        fine_h = (1, 1, 0, 1, 1, 0, 1, 0)
        gathers = {0: 1, 1: 2, 3: 1, 4: 1, 5: 2, 7: 1}
        scatters = ((0, 1), (1, 2), (1, 2), (3, 1), (4, 1), (5, 1), (6, 1), (7, 1))

        def stage_gather(e):
            if e in gathers:
                gather(e, gathers[e])

        def stage_w1(e):
            v = vector_share[e]
            groups = [(0, 1), (1, 2)] if fine[e] else [(0, 2)]
            cuts = [("S", v, MT), ("V", 0, v)]
            quantise_w1(e, [(eng, lo, hi, m0, m1) for lo, hi in groups for eng, m0, m1 in cuts if m0 < m1], len(groups))

        steps = {
            "g": stage_gather,
            "1": stage_w1,
            "2": lambda e: quantise_w2(e, "VVVVSSVV"[e]),
            "L": layer1,
            "h": lambda e: quantise_h(e, 2 if fine_h[e] else 1),
            "y": lambda e: layer2(e, *scatters[e]),
        }
        lags = {"1": 0, "2": 0, "g": 0, "L": 1, "h": 2, "y": 2}
        for i in range(E + 3):
            for step in "g21hLy":
                e = i - lags[step]
                if 0 <= e < E:
                    steps[step](e)
        nc.sync.dma_start(out, result[:])
